import numpy as np
import ml_dtypes


def mxq(x, axis, fmt="e4m3"):
    dtype, down = {"e4m3": (ml_dtypes.float8_e4m3fn, 7), "e5m2": (ml_dtypes.float8_e5m2, 14)}[fmt]
    v = np.moveaxis(np.asarray(x, np.float32).astype(ml_dtypes.bfloat16).astype(np.float64), axis, -1)
    blocks = v.reshape(v.shape[:-1] + (-1, 32))
    amax = np.abs(blocks).max(-1, keepdims=True)
    byte = np.maximum(np.where(amax > 0, np.frexp(amax)[1] - 1 + 127, 0) - down, 1)
    scale = np.exp2(byte - 127.0)
    codes = (blocks / scale).astype(np.float32).astype(dtype).astype(np.float64)
    return np.moveaxis((codes * scale).reshape(v.shape), -1, axis)


WIDE = False


def mx_kscale(k):
    if not WIDE:
        return np.ones(k)
    levels = np.array([10, -10, 5, -5, 0])
    if k % 512:
        return np.exp2(np.random.permutation(np.resize(levels, k // 32))).repeat(32)
    a = np.empty((k // 512, 16))
    for p in range(k // 512):
        a[p, :8] = np.random.permutation(np.resize(levels, 8))
        for g in range(8):
            far = levels[np.abs(levels - a[p, g]) >= 10]
            a[p, g + 8] = far[np.random.randint(len(far))]
    return np.exp2(a.ravel()).repeat(32)


def f64(x):
    return np.asarray(x).astype(np.float64)


def striped8(idx):
    return np.asarray(idx).reshape(8, -1, 16).transpose(0, 2, 1).reshape(128, -1).astype(np.uint16)


def unstriped8(offs):
    return offs.reshape(8, 16, -1).transpose(0, 2, 1).reshape(8, -1).astype(np.int64)


def pick8(x, idx, run):
    r = np.arange(len(x))
    return x[r[:, None], idx[r % (8 * run) // run]]


E2M1 = np.array([0.0, 0.5, 1.0, 1.5, 2.0, 3.0, 4.0, 6.0, -0.0, -0.5, -1.0, -1.5, -2.0, -3.0, -4.0, -6.0])


def pack_weight(w, fmt):
    k, n = w.shape
    w = f64(np.asarray(w, np.float32).astype(ml_dtypes.bfloat16)).reshape(k // 32, 32, n)
    amax = np.abs(w).max(1)
    if fmt == "e4m3":
        byte = np.frexp(amax)[1] - 1 + 127 - 7
    else:
        mant, ex = np.frexp(amax / 6.0)
        byte = np.where(mant > 0.5, ex, ex - 1) + 127
    byte = np.clip(np.where(amax > 0, byte, 1), 1, 254)
    scaled = (w * np.exp2(127.0 - byte)[:, None, :]).reshape(k, n).astype(np.float32)
    by_word = np.ascontiguousarray(scaled.reshape(k // 512, 128, 4, n).transpose(0, 1, 3, 2))
    if fmt == "e4m3":
        words = by_word.astype(ml_dtypes.float8_e4m3fn).view(np.uint8)
    else:
        c = by_word.astype(ml_dtypes.float4_e2m1fn).view(np.uint8) & 0xF
        words = (c[..., 0::2] | (c[..., 1::2] << 4)).reshape(k // 512, 128, 2 * n)
    return np.ascontiguousarray(words), np.ascontiguousarray(byte.astype(np.uint8).reshape(k // 512, 16, n))


def unpack_weight(words, scales, fmt):
    g, _, n = scales.shape
    words = np.ascontiguousarray(words).reshape(g, 128, n, -1)
    if fmt == "e4m3":
        vals = words.view(ml_dtypes.float8_e4m3fn).astype(np.float64)
    else:
        nib = np.empty((g, 128, n, 4), np.uint8)
        nib[..., 0::2] = words & 0xF
        nib[..., 1::2] = words >> 4
        vals = E2M1[nib]
    vals = vals * np.repeat(np.exp2(scales.astype(np.float64) - 127.0), 8, axis=1)[..., None]
    return vals.transpose(0, 1, 3, 2).reshape(g * 512, n)


def sigmoid(v):
    return 1.0 / (1.0 + np.exp(-v))


D, K, T, U, Z, I, Q = 512, 512, 1024, 1024, 1024, 512, 128


def setup_inputs():
    n = np.random.standard_normal
    idx = np.stack([np.random.permutation(T)[:I] for _ in range(8)])
    idx2 = np.stack([np.random.permutation(U)[:I] for _ in range(8)])
    idx3 = np.stack([np.random.permutation(Z)[:I] for _ in range(8)])
    idx4 = np.stack([np.random.permutation(Z)[:I] for _ in range(8)])
    idx5 = np.stack([np.random.permutation(Z)[:I] for _ in range(8)])
    fd = mx_kscale(D)
    fk = mx_kscale(K)
    wqp = pack_weight(n((D, K)) * 1.0 / np.sqrt(D) * fd[:, None] * fk, "e4m3")
    keysp = pack_weight(n((K, T)) * 1.0 / np.sqrt(K) / fk[:, None], "e2m1")
    notesp = pack_weight(n((D, U)) * 1.0 / np.sqrt(D) * fd[:, None], "e4m3")
    return {
        "states": (n((D, Q)) * 0.95 / fd[:, None]).astype(np.float32),
        "wq_words": wqp[0],
        "wq_scales": wqp[1],
        "keys_words": keysp[0],
        "keys_scales": keysp[1],
        "notes_words": notesp[0],
        "notes_scales": notesp[1],
        "thr": (np.random.uniform(-0.6, 0.6, (Q, 1))).astype(np.float32),
        "slope": (np.random.uniform(1.0, 3.0, (Q, 1))).astype(np.float32),
        "old": (1.0 * n((Q, Z))).astype(np.float32),
        "offs": striped8(idx),
        "offs2": striped8(idx2),
        "offs3": striped8(idx3),
        "offs4": striped8(idx4),
        "offs5": striped8(idx5),
    }


def reference(states, wq_words, wq_scales, keys_words, keys_scales, notes_words, notes_scales, thr, slope, old, offs, offs2, offs3, offs4, offs5):
    idx = unstriped8(offs)
    idx2 = unstriped8(offs2)
    idx3 = unstriped8(offs3)
    idx4 = unstriped8(offs4)
    idx5 = unstriped8(offs5)
    wqu = unpack_weight(wq_words, wq_scales, "e4m3")
    keysu = unpack_weight(keys_words, keys_scales, "e2m1")
    notesu = unpack_weight(notes_words, notes_scales, "e4m3")
    statesq = mxq(f64(states), 0, "e4m3")
    qv = wqu.T @ statesq
    qvq = mxq(qv, 0, "e4m3")
    a = qvq.T @ keysu
    b = statesq.T @ notesu
    s1 = sigmoid(pick8(a, idx, 16) * f64(slope) + f64(thr))
    s2 = sigmoid(pick8(b, idx2, 16) * f64(slope) + f64(thr))
    f1 = np.zeros((Q, Z))
    f1[np.arange(Q)[:, None], idx3[np.arange(Q) % 128 // 16]] = s1
    f2 = np.zeros((Q, Z))
    f2[np.arange(Q)[:, None], idx4[np.arange(Q) % 128 // 16]] = s2
    r = f1 - f2
    cc = f64(old) + r
    y = pick8(cc, idx5, 16)
    return y

@@ -1,0 +1,189 @@
+from contextlib import ExitStack
+
+import concourse.mybir as mybir
+
+F32 = mybir.dt.float32
+BF16 = mybir.dt.bfloat16
+I32 = mybir.dt.int32
+U32 = mybir.dt.uint32
+U16 = mybir.dt.uint16
+U8 = mybir.dt.uint8
+FP8X4 = mybir.dt.float8_e4m3fn_x4
+FP4X4 = mybir.dt.float4_e2m1fn_x4
+SIGMOID = mybir.ActivationFunctionType.Sigmoid
+COPY = mybir.ActivationFunctionType.Copy
+ADD = mybir.AluOpType.add
+SUBTRACT = mybir.AluOpType.subtract
+
+P = 128
+PACK = 4
+D, K, T, U, Z, SLOTS, Q = 512, 512, 1024, 1024, 1024, 512, 128
+PIECE = 256
+HALF = SLOTS // 2
+ROW_HALVES = (slice(0, Q // 2), slice(Q // 2, Q))
+FLOPS = 2 * Q * (D * K + K * T + D * U)
+
+
+def load_scale_rows(queue, plane, scales):
+    for quad in range(4):
+        queue.dma_start(
+            out=plane[32 * quad : 32 * quad + 4, :].bitcast(I32),
+            in_=scales[0, 4 * quad : 4 * quad + 4, :].bitcast(I32),
+        )
+
+
+def quantize_rows(nc, words, plane, values):
+    for rows in ROW_HALVES:
+        nc.vector.quantize_mx(
+            out=words[:, rows].bitcast(FP8X4), scales=plane[:, rows],
+            in_=values[:, rows, :].rearrange("p q t -> p (q t)"),
+        )
+
+
+def tile_attend_twogates_madeside_kernel(
+    tc, states, wq_words, wq_scales, keys_words, keys_scales, notes_words, notes_scales,
+    thr, slope, old, offs, offs2, offs3, offs4, offs5, out,
+):
+    nc = tc.nc
+    with ExitStack() as ctx:
+        sb = ctx.enter_context(tc.tile_pool(name="sb", bufs=1))
+        qv_pool = ctx.enter_context(tc.psum_pool(name="qv_psum", bufs=1))
+        score_pool = ctx.enter_context(tc.psum_pool(name="score_psum", bufs=4))
+
+        def list_tile(name):
+            return sb.tile([P, SLOTS // 16], U16, name=name)
+
+        token_list, note_list = list_tile("token_list"), list_tile("note_list")
+        raise_list, lower_list = list_tile("raise_list"), list_tile("lower_list")
+        read_list = list_tile("read_list")
+
+        states_raw = sb.tile([P, PACK, Q], F32)
+        notes_w = [sb.tile([P, U // 2], U32, name="notes_w%d" % h, align_bytes=64) for h in range(2)]
+        notes_s = sb.tile([P, U], U8, align_bytes=64)
+        wq_w = sb.tile([P, K], U32, align_bytes=64)
+        wq_s = sb.tile([P, K], U8, align_bytes=64)
+        keys_w = sb.tile([P, 2 * T], U8, align_bytes=64)
+        keys_s = sb.tile([P, T], U8, align_bytes=64)
+        thr_sb = sb.tile([P, 1], F32)
+        slope_sb = sb.tile([P, 1], F32)
+        old_sb = sb.tile([P, Z], F32)
+        raised = sb.tile([P, Z], F32)
+        lowered = sb.tile([P, Z], F32)
+
+        nc.vector.memset(notes_s[:].bitcast(I32), 0)
+        nc.vector.memset(wq_s[:].bitcast(I32), 0)
+        nc.vector.memset(keys_s[:].bitcast(I32), 0)
+        nc.vector.memset(lowered[:], 0.0)
+        nc.vector.memset(raised[:], 0.0)
+
+        notes_view = notes_words[0].rearrange("p n t -> p (n t)").bitcast(I32)
+        nc.gpsimd.dma_start(out=thr_sb[:], in_=thr)
+        nc.gpsimd.dma_start(out=slope_sb[:], in_=slope)
+        nc.sync.dma_start(out=states_raw[:], in_=states.rearrange("(p j) q -> p j q", j=PACK))
+        load_scale_rows(nc.scalar, notes_s, notes_scales)
+        nc.sync.dma_start(out=notes_w[0][:].bitcast(I32), in_=notes_view[:, : U // 2])
+        nc.sync.dma_start(
+            out=wq_w[:].bitcast(I32), in_=wq_words[0].rearrange("p n t -> p (n t)").bitcast(I32)
+        )
+        nc.sync.dma_start(out=notes_w[1][:].bitcast(I32), in_=notes_view[:, U // 2 :])
+        nc.sync.dma_start(note_list[:], offs2)
+        load_scale_rows(nc.scalar, wq_s, wq_scales)
+        nc.sync.dma_start(out=keys_w[:].bitcast(I32), in_=keys_words[0].bitcast(I32))
+        load_scale_rows(nc.sync, keys_s, keys_scales)
+        nc.sync.dma_start(lower_list[:], offs4)
+        nc.sync.dma_start(token_list[:], offs)
+        nc.sync.dma_start(raise_list[:], offs3)
+        nc.sync.dma_start(out=old_sb[:], in_=old)
+        nc.sync.dma_start(read_list[:], offs5)
+
+        states_bf = sb.tile([P, Q, PACK], BF16, align_bytes=64)
+        for rows in ROW_HALVES:
+            nc.vector.tensor_copy(
+                out=states_bf[:, rows, :].rearrange("p (c i) t -> p c t i", i=4),
+                in_=states_raw[:, :, rows].rearrange("p t (c i) -> p c t i", i=4),
+            )
+        states_w = sb.tile([P, Q], U32, align_bytes=64)
+        states_s = sb.tile([P, Q], U8, align_bytes=64)
+        quantize_rows(nc, states_w, states_s, states_bf)
+
+        wq_w_dealt = sb.tile([P, PACK, P], U32, tag="dealt_then_gate", align_bytes=64)
+        wq_s_dealt = sb.tile([P, PACK, P], U8, align_bytes=64)
+        nc.vector.tensor_copy(
+            out=wq_w_dealt[:].rearrange("p t m -> p m t"),
+            in_=wq_w[:].rearrange("p (m t) -> p m t", t=PACK),
+        )
+        nc.gpsimd.tensor_copy(
+            out=wq_s_dealt[:], in_=wq_s[:].rearrange("p (m t) -> p t m", t=PACK)
+        )
+
+        note_scores = sb.tile([P, U], F32)
+        for c0 in range(0, U, PIECE):
+            bank = score_pool.tile([P, PIECE], F32, name="score_bank")
+            half, within = divmod(c0, U // 2)
+            nc.tensor.matmul_mx(
+                out=bank[:],
+                lhsT=states_w[:].bitcast(FP8X4), lhsT_scale=states_s[:],
+                rhs=notes_w[half][:, within : within + PIECE].bitcast(FP8X4),
+                rhs_scale=notes_s[:, c0 : c0 + PIECE],
+                start=True, stop=True,
+            )
+            nc.vector.tensor_copy(out=note_scores[:, c0 : c0 + PIECE], in_=bank[:])
+
+        qv_bank = qv_pool.tile([P, PACK, Q], F32)
+        for t in range(PACK):
+            nc.tensor.matmul_mx(
+                out=qv_bank[:, t, :],
+                lhsT=wq_w_dealt[:, t, :].bitcast(FP8X4), lhsT_scale=wq_s_dealt[:, t, :],
+                rhs=states_w[:].bitcast(FP8X4), rhs_scale=states_s[:],
+                start=True, stop=True,
+            )
+        qv_bf = sb.tile([P, Q, PACK], BF16, align_bytes=64)
+        for rows in ROW_HALVES:
+            nc.vector.tensor_copy(
+                out=qv_bf[:, rows, :], in_=qv_bank[:, :, rows].rearrange("p t q -> p q t")
+            )
+        qv_w = sb.tile([P, Q], U32, align_bytes=64)
+        qv_s = sb.tile([P, Q], U8, align_bytes=64)
+        quantize_rows(nc, qv_w, qv_s, qv_bf)
+
+        def list_half(lists, h):
+            return lists[:, h * (HALF // 16) : (h + 1) * (HALF // 16)]
+
+        def gate_and_place(scores, score_list, places, place_list, name):
+            for h in range(2):
+                tag = "dealt_then_gate" if (name, h) == ("note_gate", 0) else "%s%d" % (name, h)
+                gate = sb.tile([P, HALF], F32, name="%s%d" % (name, h), tag=tag, align_bytes=64)
+                nc.scalar.activation(
+                    gate[:], scores[:].indirect(list_half(score_list, h)), SIGMOID,
+                    bias=thr_sb[:], scale=slope_sb[:],
+                )
+                nc.vector.tensor_copy(places[:].indirect(list_half(place_list, h)), gate[:])
+
+        gate_and_place(note_scores, note_list, lowered, lower_list, "note_gate")
+
+        token_scores = sb.tile([P, T], F32)
+        for c0 in range(0, T, PIECE):
+            bank = score_pool.tile([P, PIECE], F32, name="score_bank")
+            nc.tensor.matmul_mx(
+                out=bank[:],
+                lhsT=qv_w[:].bitcast(FP8X4), lhsT_scale=qv_s[:],
+                rhs=keys_w[:, 2 * c0 : 2 * (c0 + PIECE)].bitcast(FP4X4),
+                rhs_scale=keys_s[:, c0 : c0 + PIECE],
+                start=True, stop=True,
+            )
+            nc.scalar.copy(out=token_scores[:, c0 : c0 + PIECE], in_=bank[:])
+
+        old_lowered = sb.tile([P, Z], F32)
+        nc.gpsimd.tensor_tensor(old_lowered[:], old_sb[:], lowered[:], SUBTRACT)
+
+        gate_and_place(token_scores, token_list, raised, raise_list, "token_gate")
+
+        level = sb.tile([P, Z], F32)
+        nc.vector.tensor_tensor(level[:], old_lowered[:], raised[:], ADD)
+
+        picked0 = sb.tile([P, HALF], F32)
+        picked1 = sb.tile([P, HALF], F32)
+        nc.vector.tensor_copy(picked0[:], level[:].indirect(list_half(read_list, 0)))
+        nc.scalar.activation(picked1[:], level[:].indirect(list_half(read_list, 1)), COPY)
+        nc.sync.dma_start(out=out[:, :HALF], in_=picked0[:])
+        nc.scalar.dma_start(out=out[:, HALF:], in_=picked1[:])

@@ -70,7 +70,11 @@ def tile_attend_twogates_madeside_kernel(
         raised = sb.tile([P, Z], F32)
         lowered = sb.tile([P, Z], F32)
 
-        nc.vector.memset(notes_s[:].bitcast(I32), 0)
+        nc.gpsimd.memset(notes_s[:].bitcast(I32), 0)
+        warm_in = sb.tile([P, 1], F32)
+        warm_out = sb.tile([P, 1], F32)
+        nc.vector.memset(warm_in[:], 0.0)
+        nc.scalar.activation(warm_out[:], warm_in[:], SIGMOID)
         nc.vector.memset(wq_s[:].bitcast(I32), 0)
         nc.vector.memset(keys_s[:].bitcast(I32), 0)
         nc.vector.memset(lowered[:], 0.0)
@@ -80,14 +84,14 @@ def tile_attend_twogates_madeside_kernel(
         nc.gpsimd.dma_start(out=thr_sb[:], in_=thr)
         nc.gpsimd.dma_start(out=slope_sb[:], in_=slope)
         nc.sync.dma_start(out=states_raw[:], in_=states.rearrange("(p j) q -> p j q", j=PACK))
-        load_scale_rows(nc.scalar, notes_s, notes_scales)
-        nc.sync.dma_start(out=notes_w[0][:].bitcast(I32), in_=notes_view[:, : U // 2])
+        load_scale_rows(nc.sync, notes_s, notes_scales)
         nc.sync.dma_start(
             out=wq_w[:].bitcast(I32), in_=wq_words[0].rearrange("p n t -> p (n t)").bitcast(I32)
         )
+        nc.sync.dma_start(out=notes_w[0][:].bitcast(I32), in_=notes_view[:, : U // 2])
         nc.sync.dma_start(out=notes_w[1][:].bitcast(I32), in_=notes_view[:, U // 2 :])
+        load_scale_rows(nc.sync, wq_s, wq_scales)
         nc.sync.dma_start(note_list[:], offs2)
-        load_scale_rows(nc.scalar, wq_s, wq_scales)
         nc.sync.dma_start(out=keys_w[:].bitcast(I32), in_=keys_words[0].bitcast(I32))
         load_scale_rows(nc.sync, keys_s, keys_scales)
         nc.sync.dma_start(lower_list[:], offs4)
@@ -106,15 +110,17 @@ def tile_attend_twogates_madeside_kernel(
         states_s = sb.tile([P, Q], U8, align_bytes=64)
         quantize_rows(nc, states_w, states_s, states_bf)
 
-        wq_w_dealt = sb.tile([P, PACK, P], U32, tag="dealt_then_gate", align_bytes=64)
+        wq_w_dealt = sb.tile([P, PACK, P], U32, align_bytes=64)
         wq_s_dealt = sb.tile([P, PACK, P], U8, align_bytes=64)
         nc.vector.tensor_copy(
             out=wq_w_dealt[:].rearrange("p t m -> p m t"),
             in_=wq_w[:].rearrange("p (m t) -> p m t", t=PACK),
         )
-        nc.gpsimd.tensor_copy(
-            out=wq_s_dealt[:], in_=wq_s[:].rearrange("p (m t) -> p t m", t=PACK)
-        )
+        for pair in (slice(0, 2), slice(2, 4)):
+            nc.vector.tensor_copy(
+                out=wq_s_dealt[:, pair, :].rearrange("p t m -> p m t"),
+                in_=wq_s[:].rearrange("p (m t) -> p m t", t=PACK)[:, :, pair],
+            )
 
         note_scores = sb.tile([P, U], F32)
         for c0 in range(0, U, PIECE):
@@ -127,7 +133,7 @@ def tile_attend_twogates_madeside_kernel(
                 rhs_scale=notes_s[:, c0 : c0 + PIECE],
                 start=True, stop=True,
             )
-            nc.vector.tensor_copy(out=note_scores[:, c0 : c0 + PIECE], in_=bank[:])
+            nc.scalar.copy(out=note_scores[:, c0 : c0 + PIECE], in_=bank[:])
 
         qv_bank = qv_pool.tile([P, PACK, Q], F32)
         for t in range(PACK):
@@ -146,20 +152,17 @@ def tile_attend_twogates_madeside_kernel(
         qv_s = sb.tile([P, Q], U8, align_bytes=64)
         quantize_rows(nc, qv_w, qv_s, qv_bf)
 
+        note_gate = sb.tile([P, SLOTS], F32)
+        nc.scalar.activation(
+            note_gate[:], note_scores[:].indirect(note_list[:]), SIGMOID,
+            bias=thr_sb[:], scale=slope_sb[:],
+        )
+        nc.vector.tensor_copy(lowered[:].indirect(lower_list[:]), note_gate[:])
+        old_lowered = sb.tile([P, Z], F32)
+        nc.gpsimd.tensor_tensor(old_lowered[:], old_sb[:], lowered[:], SUBTRACT)
+
         def list_half(lists, h):
             return lists[:, h * (HALF // 16) : (h + 1) * (HALF // 16)]
-
-        def gate_and_place(scores, score_list, places, place_list, name):
-            for h in range(2):
-                tag = "dealt_then_gate" if (name, h) == ("note_gate", 0) else "%s%d" % (name, h)
-                gate = sb.tile([P, HALF], F32, name="%s%d" % (name, h), tag=tag, align_bytes=64)
-                nc.scalar.activation(
-                    gate[:], scores[:].indirect(list_half(score_list, h)), SIGMOID,
-                    bias=thr_sb[:], scale=slope_sb[:],
-                )
-                nc.vector.tensor_copy(places[:].indirect(list_half(place_list, h)), gate[:])
-
-        gate_and_place(note_scores, note_list, lowered, lower_list, "note_gate")
 
         token_scores = sb.tile([P, T], F32)
         for c0 in range(0, T, PIECE):
@@ -173,10 +176,12 @@ def tile_attend_twogates_madeside_kernel(
             )
             nc.scalar.copy(out=token_scores[:, c0 : c0 + PIECE], in_=bank[:])
 
-        old_lowered = sb.tile([P, Z], F32)
-        nc.gpsimd.tensor_tensor(old_lowered[:], old_sb[:], lowered[:], SUBTRACT)
-
-        gate_and_place(token_scores, token_list, raised, raise_list, "token_gate")
+        token_gate = sb.tile([P, SLOTS], F32)
+        nc.scalar.activation(
+            token_gate[:], token_scores[:].indirect(token_list[:]), SIGMOID,
+            bias=thr_sb[:], scale=slope_sb[:],
+        )
+        nc.vector.tensor_copy(raised[:].indirect(raise_list[:]), token_gate[:])
 
         level = sb.tile([P, Z], F32)
         nc.vector.tensor_tensor(level[:], old_lowered[:], raised[:], ADD)

from contextlib import ExitStack

import concourse.mybir as mybir

F32 = mybir.dt.float32
BF16 = mybir.dt.bfloat16
I32 = mybir.dt.int32
U32 = mybir.dt.uint32
U16 = mybir.dt.uint16
U8 = mybir.dt.uint8
FP8X4 = mybir.dt.float8_e4m3fn_x4
FP4X4 = mybir.dt.float4_e2m1fn_x4
SIGMOID = mybir.ActivationFunctionType.Sigmoid
COPY = mybir.ActivationFunctionType.Copy
ADD = mybir.AluOpType.add
SUBTRACT = mybir.AluOpType.subtract

P = 128
PACK = 4
D, K, T, U, Z, SLOTS, Q = 512, 512, 1024, 1024, 1024, 512, 128
PIECE = 256
HALF = SLOTS // 2
ROW_HALVES = (slice(0, Q // 2), slice(Q // 2, Q))
FLOPS = 2 * Q * (D * K + K * T + D * U)


def load_scale_rows(queue, plane, scales):
    for quad in range(4):
        queue.dma_start(
            out=plane[32 * quad : 32 * quad + 4, :].bitcast(I32),
            in_=scales[0, 4 * quad : 4 * quad + 4, :].bitcast(I32),
        )


def quantize_rows(nc, words, plane, values):
    for rows in ROW_HALVES:
        nc.vector.quantize_mx(
            out=words[:, rows].bitcast(FP8X4), scales=plane[:, rows],
            in_=values[:, rows, :].rearrange("p q t -> p (q t)"),
        )


def tile_attend_twogates_madeside_kernel(
    tc, states, wq_words, wq_scales, keys_words, keys_scales, notes_words, notes_scales,
    thr, slope, old, offs, offs2, offs3, offs4, offs5, out,
):
    nc = tc.nc
    with ExitStack() as ctx:
        sb = ctx.enter_context(tc.tile_pool(name="sb", bufs=1))
        qv_pool = ctx.enter_context(tc.psum_pool(name="qv_psum", bufs=1))
        score_pool = ctx.enter_context(tc.psum_pool(name="score_psum", bufs=4))

        def list_tile(name):
            return sb.tile([P, SLOTS // 16], U16, name=name)

        token_list, note_list = list_tile("token_list"), list_tile("note_list")
        raise_list, lower_list = list_tile("raise_list"), list_tile("lower_list")
        read_list = list_tile("read_list")

        states_raw = sb.tile([P, PACK, Q], F32)
        notes_w = [sb.tile([P, U // 2], U32, name="notes_w%d" % h, align_bytes=64) for h in range(2)]
        notes_s = sb.tile([P, U], U8, align_bytes=64)
        wq_w = sb.tile([P, K], U32, align_bytes=64)
        wq_s = sb.tile([P, K], U8, align_bytes=64)
        keys_w = sb.tile([P, 2 * T], U8, align_bytes=64)
        keys_s = sb.tile([P, T], U8, align_bytes=64)
        thr_sb = sb.tile([P, 1], F32)
        slope_sb = sb.tile([P, 1], F32)
        old_sb = sb.tile([P, Z], F32)
        raised = sb.tile([P, Z], F32)
        lowered = sb.tile([P, Z], F32)

        nc.gpsimd.memset(notes_s[:].bitcast(I32), 0)
        warm_in = sb.tile([P, 1], F32)
        warm_out = sb.tile([P, 1], F32)
        nc.vector.memset(warm_in[:], 0.0)
        nc.scalar.activation(warm_out[:], warm_in[:], SIGMOID)
        nc.vector.memset(wq_s[:].bitcast(I32), 0)
        nc.vector.memset(keys_s[:].bitcast(I32), 0)
        nc.vector.memset(lowered[:], 0.0)
        nc.vector.memset(raised[:], 0.0)

        notes_view = notes_words[0].rearrange("p n t -> p (n t)").bitcast(I32)
        nc.gpsimd.dma_start(out=thr_sb[:], in_=thr)
        nc.gpsimd.dma_start(out=slope_sb[:], in_=slope)
        nc.sync.dma_start(out=states_raw[:], in_=states.rearrange("(p j) q -> p j q", j=PACK))
        load_scale_rows(nc.sync, notes_s, notes_scales)
        nc.sync.dma_start(
            out=wq_w[:].bitcast(I32), in_=wq_words[0].rearrange("p n t -> p (n t)").bitcast(I32)
        )
        nc.sync.dma_start(out=notes_w[0][:].bitcast(I32), in_=notes_view[:, : U // 2])
        nc.sync.dma_start(out=notes_w[1][:].bitcast(I32), in_=notes_view[:, U // 2 :])
        load_scale_rows(nc.sync, wq_s, wq_scales)
        nc.sync.dma_start(note_list[:], offs2)
        nc.sync.dma_start(out=keys_w[:].bitcast(I32), in_=keys_words[0].bitcast(I32))
        load_scale_rows(nc.sync, keys_s, keys_scales)
        nc.sync.dma_start(lower_list[:], offs4)
        nc.sync.dma_start(token_list[:], offs)
        nc.sync.dma_start(raise_list[:], offs3)
        nc.sync.dma_start(out=old_sb[:], in_=old)
        nc.sync.dma_start(read_list[:], offs5)

        states_bf = sb.tile([P, Q, PACK], BF16, align_bytes=64)
        for rows in ROW_HALVES:
            nc.vector.tensor_copy(
                out=states_bf[:, rows, :].rearrange("p (c i) t -> p c t i", i=4),
                in_=states_raw[:, :, rows].rearrange("p t (c i) -> p c t i", i=4),
            )
        states_w = sb.tile([P, Q], U32, align_bytes=64)
        states_s = sb.tile([P, Q], U8, align_bytes=64)
        quantize_rows(nc, states_w, states_s, states_bf)

        wq_w_dealt = sb.tile([P, PACK, P], U32, align_bytes=64)
        wq_s_dealt = sb.tile([P, PACK, P], U8, align_bytes=64)
        nc.vector.tensor_copy(
            out=wq_w_dealt[:].rearrange("p t m -> p m t"),
            in_=wq_w[:].rearrange("p (m t) -> p m t", t=PACK),
        )
        for pair in (slice(0, 2), slice(2, 4)):
            nc.vector.tensor_copy(
                out=wq_s_dealt[:, pair, :].rearrange("p t m -> p m t"),
                in_=wq_s[:].rearrange("p (m t) -> p m t", t=PACK)[:, :, pair],
            )

        note_scores = sb.tile([P, U], F32)
        for c0 in range(0, U, PIECE):
            bank = score_pool.tile([P, PIECE], F32, name="score_bank")
            half, within = divmod(c0, U // 2)
            nc.tensor.matmul_mx(
                out=bank[:],
                lhsT=states_w[:].bitcast(FP8X4), lhsT_scale=states_s[:],
                rhs=notes_w[half][:, within : within + PIECE].bitcast(FP8X4),
                rhs_scale=notes_s[:, c0 : c0 + PIECE],
                start=True, stop=True,
            )
            nc.scalar.copy(out=note_scores[:, c0 : c0 + PIECE], in_=bank[:])

        qv_bank = qv_pool.tile([P, PACK, Q], F32)
        for t in range(PACK):
            nc.tensor.matmul_mx(
                out=qv_bank[:, t, :],
                lhsT=wq_w_dealt[:, t, :].bitcast(FP8X4), lhsT_scale=wq_s_dealt[:, t, :],
                rhs=states_w[:].bitcast(FP8X4), rhs_scale=states_s[:],
                start=True, stop=True,
            )
        qv_bf = sb.tile([P, Q, PACK], BF16, align_bytes=64)
        for rows in ROW_HALVES:
            nc.vector.tensor_copy(
                out=qv_bf[:, rows, :], in_=qv_bank[:, :, rows].rearrange("p t q -> p q t")
            )
        qv_w = sb.tile([P, Q], U32, align_bytes=64)
        qv_s = sb.tile([P, Q], U8, align_bytes=64)
        quantize_rows(nc, qv_w, qv_s, qv_bf)

        note_gate = sb.tile([P, SLOTS], F32)
        nc.scalar.activation(
            note_gate[:], note_scores[:].indirect(note_list[:]), SIGMOID,
            bias=thr_sb[:], scale=slope_sb[:],
        )
        nc.vector.tensor_copy(lowered[:].indirect(lower_list[:]), note_gate[:])
        old_lowered = sb.tile([P, Z], F32)
        nc.gpsimd.tensor_tensor(old_lowered[:], old_sb[:], lowered[:], SUBTRACT)

        def list_half(lists, h):
            return lists[:, h * (HALF // 16) : (h + 1) * (HALF // 16)]

        token_scores = sb.tile([P, T], F32)
        for c0 in range(0, T, PIECE):
            bank = score_pool.tile([P, PIECE], F32, name="score_bank")
            nc.tensor.matmul_mx(
                out=bank[:],
                lhsT=qv_w[:].bitcast(FP8X4), lhsT_scale=qv_s[:],
                rhs=keys_w[:, 2 * c0 : 2 * (c0 + PIECE)].bitcast(FP4X4),
                rhs_scale=keys_s[:, c0 : c0 + PIECE],
                start=True, stop=True,
            )
            nc.scalar.copy(out=token_scores[:, c0 : c0 + PIECE], in_=bank[:])

        token_gate = sb.tile([P, SLOTS], F32)
        nc.scalar.activation(
            token_gate[:], token_scores[:].indirect(token_list[:]), SIGMOID,
            bias=thr_sb[:], scale=slope_sb[:],
        )
        nc.vector.tensor_copy(raised[:].indirect(raise_list[:]), token_gate[:])

        level = sb.tile([P, Z], F32)
        nc.vector.tensor_tensor(level[:], old_lowered[:], raised[:], ADD)

        picked0 = sb.tile([P, HALF], F32)
        picked1 = sb.tile([P, HALF], F32)
        nc.vector.tensor_copy(picked0[:], level[:].indirect(list_half(read_list, 0)))
        nc.scalar.activation(picked1[:], level[:].indirect(list_half(read_list, 1)), COPY)
        nc.sync.dma_start(out=out[:, :HALF], in_=picked0[:])
        nc.scalar.dma_start(out=out[:, HALF:], in_=picked1[:])
